import numpy as np
import ml_dtypes


def mxq(x, axis, fmt="e4m3"):
    dtype, down = {"e4m3": (ml_dtypes.float8_e4m3fn, 7), "e5m2": (ml_dtypes.float8_e5m2, 14)}[fmt]
    v = np.moveaxis(np.asarray(x, np.float32).astype(ml_dtypes.bfloat16).astype(np.float64), axis, -1)
    blocks = v.reshape(v.shape[:-1] + (-1, 32))
    amax = np.abs(blocks).max(-1, keepdims=True)
    byte = np.maximum(np.where(amax > 0, np.frexp(amax)[1] - 1 + 127, 0) - down, 1)
    scale = np.exp2(byte - 127.0)
    codes = (blocks / scale).astype(np.float32).astype(dtype).astype(np.float64)
    return np.moveaxis((codes * scale).reshape(v.shape), -1, axis)


WIDE = False


def mx_kscale(k):
    if not WIDE:
        return np.ones(k)
    levels = np.array([10, -10, 5, -5, 0])
    if k % 512:
        return np.exp2(np.random.permutation(np.resize(levels, k // 32))).repeat(32)
    a = np.empty((k // 512, 16))
    for p in range(k // 512):
        a[p, :8] = np.random.permutation(np.resize(levels, 8))
        for g in range(8):
            far = levels[np.abs(levels - a[p, g]) >= 10]
            a[p, g + 8] = far[np.random.randint(len(far))]
    return np.exp2(a.ravel()).repeat(32)


def f64(x):
    return np.asarray(x).astype(np.float64)


def striped(idx):
    return np.tile(idx.reshape(-1, 16).T, (8, 1)).astype(np.uint16)


def unstriped(offs):
    return offs[:16].T.reshape(-1).astype(np.int64)


E2M1 = np.array([0.0, 0.5, 1.0, 1.5, 2.0, 3.0, 4.0, 6.0, -0.0, -0.5, -1.0, -1.5, -2.0, -3.0, -4.0, -6.0])


def pack_weight(w, fmt):
    k, n = w.shape
    w = f64(np.asarray(w, np.float32).astype(ml_dtypes.bfloat16)).reshape(k // 32, 32, n)
    amax = np.abs(w).max(1)
    if fmt == "e4m3":
        byte = np.frexp(amax)[1] - 1 + 127 - 7
    else:
        mant, ex = np.frexp(amax / 6.0)
        byte = np.where(mant > 0.5, ex, ex - 1) + 127
    byte = np.clip(np.where(amax > 0, byte, 1), 1, 254)
    scaled = (w * np.exp2(127.0 - byte)[:, None, :]).reshape(k, n).astype(np.float32)
    by_word = np.ascontiguousarray(scaled.reshape(k // 512, 128, 4, n).transpose(0, 1, 3, 2))
    if fmt == "e4m3":
        words = by_word.astype(ml_dtypes.float8_e4m3fn).view(np.uint8)
    else:
        c = by_word.astype(ml_dtypes.float4_e2m1fn).view(np.uint8) & 0xF
        words = (c[..., 0::2] | (c[..., 1::2] << 4)).reshape(k // 512, 128, 2 * n)
    return np.ascontiguousarray(words), np.ascontiguousarray(byte.astype(np.uint8).reshape(k // 512, 16, n))


def unpack_weight(words, scales, fmt):
    g, _, n = scales.shape
    words = np.ascontiguousarray(words).reshape(g, 128, n, -1)
    if fmt == "e4m3":
        vals = words.view(ml_dtypes.float8_e4m3fn).astype(np.float64)
    else:
        nib = np.empty((g, 128, n, 4), np.uint8)
        nib[..., 0::2] = words & 0xF
        nib[..., 1::2] = words >> 4
        vals = E2M1[nib]
    vals = vals * np.repeat(np.exp2(scales.astype(np.float64) - 127.0), 8, axis=1)[..., None]
    return vals.transpose(0, 1, 3, 2).reshape(g * 512, n)


def gelu(v):
    return 0.5 * v * (1.0 + np.tanh(np.sqrt(2.0 / np.pi) * (v + 0.044715 * v**3)))


K, H, N, T, S, T2, P = 1024, 512, 256, 2048, 1024, 2048, 1024

def setup_inputs():
    n = np.random.standard_normal
    s, u = mx_kscale(K)[:, None], mx_kscale(H)[:, None]
    tab_words, tab_scales = pack_weight(n((K, T)) * s, "e4m3")
    w2_words, w2_scales = pack_weight(0.7 * n((K, H)) / np.sqrt(K) / s, "e2m1")
    w4_words, w4_scales = pack_weight(n((H, N)) / np.sqrt(H) / u, "e4m3")
    return {
        "tab_words": tab_words, "tab_scales": tab_scales,
        "offs": striped(np.random.permutation(T)[:S]),
        "offs2": striped(np.random.permutation(T2)[:S]),
        "offs3": striped(np.random.permutation(T2)[:P]),
        "offs4": striped(np.random.permutation(T2)[:P]),
        "w1": (2.0 * n((K, H)) / np.sqrt(K) / s).astype(np.float32),
        "w2_words": w2_words, "w2_scales": w2_scales,
        "gain": (np.exp(0.4 * n(H)) * u[:, 0]).astype(np.float32),
        "wgs": np.exp(0.3 * n((128, S))).astype(np.float32),
        "page0": (n((H, T2)) * u).astype(np.float32),
        "decay": (0.8 * np.exp(0.4 * n(H))).astype(np.float32),
        "w3": (1.3 * n((H, H)) / np.sqrt(H) / u).astype(np.float32),
        "gain2": (1.2 * np.exp(0.4 * n(H)) * u[:, 0]).astype(np.float32),
        "w4_words": w4_words, "w4_scales": w4_scales,
    }

def reference(tab_words, tab_scales, offs, offs2, offs3, offs4, w1, w2_words, w2_scales, gain, wgs, page0, decay, w3, gain2, w4_words, w4_scales):
    v = unpack_weight(tab_words, tab_scales, "e4m3")[:, unstriped(offs)]
    w2 = unpack_weight(w2_words, w2_scales, "e2m1")
    w4 = unpack_weight(w4_words, w4_scales, "e4m3")
    bent = np.tanh(mxq(f64(w1), 0, "e4m3").T @ v)
    h = f64(gain)[:, None] * (bent + (w2.T @ v))
    before = f64(page0)
    page = before.copy()
    page[:, unstriped(offs2)] = np.tile(f64(wgs), (H // 128, 1)) * h
    x = np.maximum(page[:, unstriped(offs3)], f64(decay)[:, None] * before[:, unstriped(offs4)])
    y = mxq(f64(w3), 0, "e4m3").T @ mxq(x, 0, "e4m3")
    gelu = 0.5 * y * (1.0 + np.tanh(0.7978845608 * (y + 0.044715 * y ** 3)))
    z = f64(gain2)[:, None] * gelu + x
    return w4.T @ mxq(z, 0, "e4m3")

@@ -1,0 +1,312 @@
+from contextlib import ExitStack
+
+import concourse.mybir as mybir
+from concourse.masks import make_identity
+
+K, H, N, T, S, T2, PJ = 1024, 512, 256, 2048, 1024, 2048, 1024
+FLOPS = 2952790016
+
+F32 = mybir.dt.float32
+BF16 = mybir.dt.bfloat16
+I32 = mybir.dt.int32
+U32 = mybir.dt.uint32
+U16 = mybir.dt.uint16
+U8 = mybir.dt.uint8
+FP8X4 = mybir.dt.float8_e4m3fn_x4
+FP4X4 = mybir.dt.float4_e2m1fn_x4
+ALU = mybir.AluOpType
+ACT = mybir.ActivationFunctionType
+
+P = 128
+PACK = 4
+PASSES = K // (P * PACK)
+CHUNK = 256
+CHUNKS = PJ // CHUNK
+LIST_ROWS = 16
+
+
+def weave(copy, dst, src):
+    copy(
+        out=dst.rearrange("p (c k i) -> p c i k", k=4, i=PACK),
+        in_=src.rearrange("p i (c k) -> p c i k", k=4),
+    )
+
+
+def tile_list_embankment_regrowth_scores_kernel(
+    tc, tab_words, tab_scales, offs, offs2, offs3, offs4, w1, w2_words, w2_scales,
+    gain, wgs, page0, decay, w3, gain2, w4_words, w4_scales, out,
+):
+    nc = tc.nc
+    with ExitStack() as ctx:
+        keep = ctx.enter_context(tc.tile_pool(name="keep", bufs=1))
+        psum = ctx.enter_context(tc.psum_pool(name="psum", bufs=4))
+
+        def tile(shape, dtype, name, tag=None, bufs=None):
+            return keep.tile(shape, dtype, name=name, tag=tag or name, bufs=bufs, align_bytes=64)
+
+        def load_list(src, name):
+            lst = tile([P, S // LIST_ROWS], U16, name)
+            nc.sync.dma_start(lst[:], src)
+            return lst
+
+        def entries(lst, first, count):
+            return lst[:, first // LIST_ROWS : (first + count) // LIST_ROWS]
+
+        idx = load_list(offs, "idx")
+        tab_s = tile([P, T], U8, "tab_s")
+        nc.vector.memset(tab_s[:].bitcast(I32), 0)
+        tab_w = [tile([P, T], U32, f"tab_w{a}") for a in range(PASSES)]
+
+        def load_words(a):
+            nc.sync.dma_start(
+                tab_w[a][:].bitcast(I32), tab_words[a].rearrange("p n i -> p (n i)").bitcast(I32)
+            )
+
+        load_words(0)
+        for q in range(4):
+            nc.scalar.dma_start(
+                tab_s[32 * q : 32 * q + 8, :].bitcast(I32),
+                tab_scales[:, 4 * q : 4 * q + 4, :].bitcast(I32),
+            )
+        load_words(1)
+        w2_w = tile([P, PASSES, 2 * H], U8, "w2_w")
+        nc.sync.dma_start(w2_w[:].bitcast(I32), w2_words.rearrange("a p c -> p a c").bitcast(I32))
+        w2_s = tile([P, PASSES, H], U8, "w2_s")
+        nc.gpsimd.memset(w2_s[:].bitcast(I32), 0)
+        for q in range(4):
+            nc.scalar.dma_start(
+                w2_s[32 * q : 32 * q + 4].bitcast(I32),
+                w2_scales[:, 4 * q : 4 * q + 4, :].rearrange("a r c -> r a c").bitcast(I32),
+            )
+        v_s1 = tile([P, S], U8, "v_s1")
+        nc.gpsimd.memset(v_s1[:].bitcast(I32), 0)
+        ident = tile([P, P], F32, "ident")
+        make_identity(nc, ident[:])
+
+        halves = [slice(0, H // 2), slice(H // 2, H)]
+        w1_raw = [[tile([P, PACK, H // 2], F32, f"w1_raw{a}{u}") for u in range(2)] for a in range(PASSES)]
+        for a in range(PASSES):
+            rows = w1[512 * a : 512 * (a + 1), :].rearrange("(p i) c -> p i c", i=PACK)
+            for u in range(2):
+                nc.sync.dma_start(w1_raw[a][u][:], rows[:, :, halves[u]])
+
+        def load_vector(src, name):
+            vec = tile([P, PACK], F32, name)
+            nc.sync.dma_start(vec[:], src.rearrange("(p t) -> p t", t=PACK))
+            return vec
+
+        gain_v = load_vector(gain, "gain_v")
+        idx4 = load_list(offs4, "idx4")
+        idx2 = load_list(offs2, "idx2")
+        page = [tile([P, T2], F32, f"page{t}") for t in range(PACK)]
+        wg = [tile([P, S], F32, f"wg{t}") for t in range(PACK)]
+        page_rows = page0.rearrange("(p t) c -> t p c", t=PACK)
+        wgs_rows = wgs.rearrange("(p t) j -> t p j", t=PACK)
+        for t in range(PACK):
+            nc.sync.dma_start(page[t][:], page_rows[t])
+            for q in (0, 2, 1, 3):
+                nc.sync.dma_start(wg[t][32 * q : 32 * (q + 1), :], wgs_rows[t])
+        idx3 = load_list(offs3, "idx3")
+        decay_v = load_vector(decay, "decay_v")
+        gain2_v = load_vector(gain2, "gain2_v")
+        w3_raw = tile([P, PACK, H], F32, "w3_raw")
+        nc.sync.dma_start(w3_raw[:], w3.rearrange("(p i) m -> p i m", i=PACK))
+        w4_w = tile([P, N], U32, "w4_w")
+        nc.sync.dma_start(w4_w[:].bitcast(I32), w4_words[0].rearrange("p n i -> p (n i)").bitcast(I32))
+        w4_s = tile([P, N], U8, "w4_s")
+        nc.gpsimd.memset(w4_s[:].bitcast(I32), 0)
+        for q in range(4):
+            nc.sync.dma_start(
+                w4_s[32 * q : 32 * q + 4, :].bitcast(I32),
+                w4_scales[0, 4 * q : 4 * q + 4, :].bitcast(I32),
+            )
+
+        v_s0 = tile([P, S], U8, "v_s0")
+        nc.vector.tensor_copy(v_s0[:], tab_s[:].indirect(idx[:]))
+        for q in range(4):
+            nc.scalar.dma_start(
+                v_s1[32 * q : 32 * q + 4, :].bitcast(I32),
+                v_s0[32 * q + 4 : 32 * q + 8, :].bitcast(I32),
+            )
+        v_s = [v_s0, v_s1]
+        v_w = [tile([P, S], U32, f"v_w{a}") for a in range(PASSES)]
+        for a in range(PASSES):
+            for j0 in range(0, S, 512):
+                nc.vector.tensor_copy(
+                    v_w[a][:, j0 : j0 + 512], tab_w[a][:].indirect(entries(idx, j0, 512))
+                )
+
+        def product(acc, jt, words, scales):
+            cols = slice(P * jt, P * (jt + 1))
+            for a in range(PASSES):
+                nc.tensor.matmul_mx(
+                    out=acc[:], lhsT=v_w[a][:, cols].bitcast(FP8X4), lhsT_scale=v_s[a][:, cols],
+                    rhs=words[a], rhs_scale=scales[a], start=(a == 0), stop=(a == PASSES - 1),
+                )
+
+        w1_w = [tile([P, H], U32, f"w1_w{a}") for a in range(PASSES)]
+        w1_s = [tile([P, H], U8, f"w1_s{a}") for a in range(PASSES)]
+        for a in range(PASSES):
+            for u in range(2):
+                w1_b = tile([P, H // 2 * PACK], BF16, f"w1_b{a}{u}")
+                weave(nc.vector.tensor_copy, w1_b[:], w1_raw[a][u][:])
+                nc.vector.quantize_mx(
+                    out=w1_w[a][:, halves[u]].bitcast(FP8X4), scales=w1_s[a][:, halves[u]], in_=w1_b[:]
+                )
+
+        h = [tile([P, S], F32, f"h{t}") for t in range(PACK)]
+        for c in range(CHUNKS):
+            lin, bent = [], []
+            for jj in range(2):
+                acc = psum.tile([P, H], F32, name="lin_acc", tag="mm0", bufs=2)
+                product(acc, 2 * c + jj, [w2_w[:, a, :].bitcast(FP4X4) for a in range(PASSES)],
+                        [w2_s[:, a, :] for a in range(PASSES)])
+                lin_t = tile([P, PACK, P], F32, f"lin{c}{jj}")
+                nc.scalar.activation(
+                    out=lin_t[:], in_=acc[:].rearrange("j (p t) -> j t p", t=PACK), func=ACT.Copy
+                )
+                lin.append(lin_t)
+            for jj in range(2):
+                acc = psum.tile([P, H], F32, name="bent_acc", tag="mm1", bufs=2)
+                product(acc, 2 * c + jj, [w1_w[a][:].bitcast(FP8X4) for a in range(PASSES)],
+                        [w1_s[a][:] for a in range(PASSES)])
+                bent_t = tile([P, PACK, P], F32, "bent", bufs=4)
+                nc.scalar.activation(
+                    out=bent_t[:], in_=acc[:].rearrange("j (p t) -> j t p", t=PACK), func=ACT.Tanh
+                )
+                bent.append(bent_t)
+            for pair in range(2):
+                bank = psum.tile([P, 2, CHUNK], F32, name="h_acc", tag="tr")
+                for tt in range(2):
+                    t = 2 * pair + tt
+                    for jj in range(2):
+                        dst = bank[:, tt, P * jj : P * (jj + 1)]
+                        nc.tensor.matmul(dst, lin[jj][:, t, :], ident[:],
+                                         start=True, stop=False, is_transpose=True)
+                        nc.tensor.matmul(dst, bent[jj][:, t, :], ident[:],
+                                         start=False, stop=True, is_transpose=True)
+                for tt in range(2):
+                    t = 2 * pair + tt
+                    nc.scalar.activation(
+                        out=h[t][:, CHUNK * c : CHUNK * (c + 1)], in_=bank[:, tt, :],
+                        func=ACT.Copy, scale=gain_v[:, t : t + 1],
+                    )
+
+        old = [tile([P, PJ], F32, f"old{t}") for t in range(PACK)]
+        def read_old(t):
+            nc.vector.tensor_copy(old[t][:], page[t][:].indirect(idx4[:]))
+
+        def put(t, first, count):
+            cols = slice(first, first + count)
+            nc.vector.tensor_tensor(
+                page[t][:].indirect(entries(idx2, first, count)), h[t][:, cols], wg[t][:, cols], ALU.mult
+            )
+
+        read_old(0)
+        put(0, 0, 256)
+        read_old(1)
+        put(0, 256, 256)
+        put(1, 0, 512)
+        read_old(2)
+        put(0, 512, 512)
+        put(1, 512, 512)
+        put(2, 0, 1024)
+        read_old(3)
+        put(3, 0, 1024)
+
+        w3_b = tile([P, H * PACK], BF16, "w3_b")
+        nc.scalar.copy(
+            out=w3_b[:].rearrange("p (t m i) -> p t m i", t=PACK, i=PACK),
+            in_=w3_raw[:].rearrange("p i (m t) -> p t m i", t=PACK),
+        )
+        w3_w = tile([P, H], U32, "w3_w")
+        w3_s = tile([P, H], U8, "w3_s")
+        nc.vector.quantize_mx(out=w3_w[:].bitcast(FP8X4), scales=w3_s[:], in_=w3_b[:])
+
+        out_rows = out.rearrange("(a p) j -> p a j", p=P)
+        new, x, x_b, x_q, g, z, z_b = {}, {}, {}, {}, {}, {}, {}
+
+        def new_tag(c, t):
+            if c == 0:
+                return "new_b" if t == 3 else f"first{t}"
+            if t == 0:
+                return "h3" if c == 1 else f"g{c % 2}"
+            return {1: "new_b", 2: "x_b", 3: "z_b"}[t]
+
+        def read_new(c, t):
+            new[c, t] = tile([P, CHUNK], F32, f"new{c}{t}", tag=new_tag(c, t))
+            nc.vector.tensor_copy(new[c, t][:], page[t][:].indirect(entries(idx3, CHUNK * c, CHUNK)))
+
+        def weave_engine(c):
+            return nc.vector.tensor_copy if c == CHUNKS - 1 else nc.scalar.copy
+
+        def make_x(c):
+            cols = slice(CHUNK * c, CHUNK * (c + 1))
+            x[c] = tile([P, PACK, CHUNK], F32, f"x{c}")
+            for t in range(PACK):
+                nc.vector.scalar_tensor_tensor(
+                    x[c][:, t, :], old[t][:, cols], decay_v[:, t : t + 1], new[c, t][:], ALU.mult, ALU.max
+                )
+            x_b[c] = tile([P, CHUNK * PACK], BF16, f"x_b{c}", tag="x_b")
+            weave(weave_engine(c), x_b[c][:], x[c][:])
+
+        def quantise(woven, name):
+            words = tile([P, CHUNK], U32, name + "_w", bufs=2)
+            scales = tile([P, CHUNK], U8, name + "_s", bufs=2)
+            nc.vector.quantize_mx(out=words[:].bitcast(FP8X4), scales=scales[:], in_=woven[:])
+            return words, scales
+
+        def stage_y(c):
+            x_w, x_s = quantise(x_b[c], "x")
+            g[c] = tile([P, PACK, CHUNK], F32, f"g{c}", tag=f"g{c % 2}")
+            for pair in range(2):
+                bank = psum.tile([P, 2, CHUNK], F32, name="y_acc", tag=f"mm{pair}", bufs=2)
+                for tt in range(2):
+                    m = slice(P * (2 * pair + tt), P * (2 * pair + tt + 1))
+                    nc.tensor.matmul_mx(
+                        out=bank[:, tt, :], lhsT=w3_w[:, m].bitcast(FP8X4), lhsT_scale=w3_s[:, m],
+                        rhs=x_w[:].bitcast(FP8X4), rhs_scale=x_s[:], start=True, stop=True,
+                    )
+                nc.scalar.activation(
+                    out=g[c][:, 2 * pair : 2 * pair + 2, :], in_=bank[:], func=ACT.Gelu_apprx_tanh
+                )
+
+        def make_z(c):
+            z[c] = tile([P, PACK, CHUNK], BF16, "z", bufs=2)
+            for t in range(PACK):
+                nc.vector.scalar_tensor_tensor(
+                    z[c][:, t, :], g[c][:, t, :], gain2_v[:, t : t + 1], x[c][:, t, :], ALU.mult, ALU.add
+                )
+            z_b[c] = tile([P, CHUNK * PACK], BF16, f"z_b{c}", tag=("z_last" if c == CHUNKS - 1 else "z_b"))
+            weave(weave_engine(c), z_b[c][:], z[c][:])
+
+        def stage_out(c):
+            z_w, z_s = quantise(z_b[c], "z")
+            bank = psum.tile([P, N // P, CHUNK], F32, name="out_acc", tag="tr")
+            for a in range(N // P):
+                n = slice(P * a, P * (a + 1))
+                nc.tensor.matmul_mx(
+                    out=bank[:, a, :], lhsT=w4_w[:, n].bitcast(FP8X4), lhsT_scale=w4_s[:, n],
+                    rhs=z_w[:].bitcast(FP8X4), rhs_scale=z_s[:], start=True, stop=True,
+                )
+            res = tile([P, N // P, CHUNK], F32, "res", bufs=2)
+            nc.scalar.copy(out=res[:], in_=bank[:])
+            nc.sync.dma_start(out_rows[:, :, CHUNK * c : CHUNK * (c + 1)], res[:])
+
+        for t in range(PACK):
+            read_new(0, t)
+        make_x(0)
+        for c in range(1, CHUNKS):
+            read_new(c, 0)
+            read_new(c, 1)
+            stage_y(c - 1)
+            read_new(c, 2)
+            if c >= 2:
+                stage_out(c - 2)
+            read_new(c, 3)
+            make_x(c)
+            make_z(c - 1)
+        stage_y(CHUNKS - 1)
+        stage_out(CHUNKS - 2)
+        make_z(CHUNKS - 1)
+        stage_out(CHUNKS - 1)

@@ -23,6 +23,7 @@ PASSES = K // (P * PACK)
 CHUNK = 256
 CHUNKS = PJ // CHUNK
 LIST_ROWS = 16
+IN_PAGE = 2
 
 
 def weave(copy, dst, src):
@@ -54,7 +55,13 @@ def tile_list_embankment_regrowth_scores_kernel(
 
         idx = load_list(offs, "idx")
         tab_s = tile([P, T], U8, "tab_s")
-        nc.vector.memset(tab_s[:].bitcast(I32), 0)
+        scale_rows = tab_scales.rearrange("a q t -> (a q) t").bitcast(I32)
+        nc.sync.dma_start(tab_s[0:32, :].bitcast(I32), scale_rows)
+        for q in range(1, 4):
+            nc.sync.dma_start(
+                tab_s[32 * q : 32 * (q + 1), :].bitcast(I32),
+                scale_rows[4 * q : 4 * q + 4, :].unsqueeze(0).to_broadcast([8, 4, T // 4]),
+            )
         tab_w = [tile([P, T], U32, f"tab_w{a}") for a in range(PASSES)]
 
         def load_words(a):
@@ -62,30 +69,10 @@ def tile_list_embankment_regrowth_scores_kernel(
                 tab_w[a][:].bitcast(I32), tab_words[a].rearrange("p n i -> p (n i)").bitcast(I32)
             )
 
-        load_words(0)
-        for q in range(4):
-            nc.scalar.dma_start(
-                tab_s[32 * q : 32 * q + 8, :].bitcast(I32),
-                tab_scales[:, 4 * q : 4 * q + 4, :].bitcast(I32),
-            )
-        load_words(1)
-        w2_w = tile([P, PASSES, 2 * H], U8, "w2_w")
-        nc.sync.dma_start(w2_w[:].bitcast(I32), w2_words.rearrange("a p c -> p a c").bitcast(I32))
-        w2_s = tile([P, PASSES, H], U8, "w2_s")
-        nc.gpsimd.memset(w2_s[:].bitcast(I32), 0)
-        for q in range(4):
-            nc.scalar.dma_start(
-                w2_s[32 * q : 32 * q + 4].bitcast(I32),
-                w2_scales[:, 4 * q : 4 * q + 4, :].rearrange("a r c -> r a c").bitcast(I32),
-            )
-        v_s1 = tile([P, S], U8, "v_s1")
-        nc.gpsimd.memset(v_s1[:].bitcast(I32), 0)
-        ident = tile([P, P], F32, "ident")
-        make_identity(nc, ident[:])
-
         halves = [slice(0, H // 2), slice(H // 2, H)]
         w1_raw = [[tile([P, PACK, H // 2], F32, f"w1_raw{a}{u}") for u in range(2)] for a in range(PASSES)]
-        for a in range(PASSES):
+
+        def load_w1(a):
             rows = w1[512 * a : 512 * (a + 1), :].rearrange("(p i) c -> p i c", i=PACK)
             for u in range(2):
                 nc.sync.dma_start(w1_raw[a][u][:], rows[:, :, halves[u]])
@@ -95,38 +82,32 @@ def tile_list_embankment_regrowth_scores_kernel(
             nc.sync.dma_start(vec[:], src.rearrange("(p t) -> p t", t=PACK))
             return vec
 
-        gain_v = load_vector(gain, "gain_v")
-        idx4 = load_list(offs4, "idx4")
-        idx2 = load_list(offs2, "idx2")
-        page = [tile([P, T2], F32, f"page{t}") for t in range(PACK)]
-        wg = [tile([P, S], F32, f"wg{t}") for t in range(PACK)]
-        page_rows = page0.rearrange("(p t) c -> t p c", t=PACK)
-        wgs_rows = wgs.rearrange("(p t) j -> t p j", t=PACK)
-        for t in range(PACK):
-            nc.sync.dma_start(page[t][:], page_rows[t])
-            for q in (0, 2, 1, 3):
-                nc.sync.dma_start(wg[t][32 * q : 32 * (q + 1), :], wgs_rows[t])
-        idx3 = load_list(offs3, "idx3")
-        decay_v = load_vector(decay, "decay_v")
-        gain2_v = load_vector(gain2, "gain2_v")
-        w3_raw = tile([P, PACK, H], F32, "w3_raw")
-        nc.sync.dma_start(w3_raw[:], w3.rearrange("(p i) m -> p i m", i=PACK))
-        w4_w = tile([P, N], U32, "w4_w")
-        nc.sync.dma_start(w4_w[:].bitcast(I32), w4_words[0].rearrange("p n i -> p (n i)").bitcast(I32))
-        w4_s = tile([P, N], U8, "w4_s")
-        nc.gpsimd.memset(w4_s[:].bitcast(I32), 0)
+        load_words(0)
+        load_w1(0)
+        load_words(1)
+        w2_s = tile([P, PASSES, H], U8, "w2_s")
+        nc.vector.memset(w2_s[:].bitcast(I32), 0)
         for q in range(4):
             nc.sync.dma_start(
-                w4_s[32 * q : 32 * q + 4, :].bitcast(I32),
-                w4_scales[0, 4 * q : 4 * q + 4, :].bitcast(I32),
+                w2_s[32 * q : 32 * q + 4].bitcast(I32),
+                w2_scales[:, 4 * q : 4 * q + 4, :].rearrange("a r c -> r a c").bitcast(I32),
             )
+        w2_w = tile([P, PASSES, 2 * H], U8, "w2_w")
+        nc.sync.dma_start(w2_w[:].bitcast(I32), w2_words.rearrange("a p c -> p a c").bitcast(I32))
+        v_s1 = tile([P, S], U8, "v_s1")
+        nc.vector.memset(v_s1[:].bitcast(I32), 0)
+        w4_s = tile([P, N], U8, "w4_s")
+        nc.vector.memset(w4_s[:].bitcast(I32), 0)
+        ident = tile([P, P], F32, "ident")
+        make_identity(nc, ident[:])
+        load_w1(1)
 
         v_s0 = tile([P, S], U8, "v_s0")
         nc.vector.tensor_copy(v_s0[:], tab_s[:].indirect(idx[:]))
         for q in range(4):
-            nc.scalar.dma_start(
+            nc.gpsimd.dma_start(
                 v_s1[32 * q : 32 * q + 4, :].bitcast(I32),
-                v_s0[32 * q + 4 : 32 * q + 8, :].bitcast(I32),
+                v_s0[16 + 4 * q : 16 + 4 * q + 4, :].bitcast(I32),
             )
         v_s = [v_s0, v_s1]
         v_w = [tile([P, S], U32, f"v_w{a}") for a in range(PASSES)]
@@ -135,6 +116,38 @@ def tile_list_embankment_regrowth_scores_kernel(
                 nc.vector.tensor_copy(
                     v_w[a][:, j0 : j0 + 512], tab_w[a][:].indirect(entries(idx, j0, 512))
                 )
+
+        page = [tile([P, T2], F32, f"page{t}") for t in range(PACK)]
+        wg = [tile([P, S], F32, f"wg{t}") for t in range(PACK)]
+        page_rows = page0.rearrange("(p t) c -> t p c", t=PACK)
+        wgs_rows = wgs.rearrange("(p t) j -> t p j", t=PACK)
+
+        def load_page(t):
+            nc.sync.dma_start(page[t][:], page_rows[t])
+            for q in (0, 2, 1, 3):
+                nc.sync.dma_start(wg[t][32 * q : 32 * (q + 1), :], wgs_rows[t])
+
+        idx4 = load_list(offs4, "idx4")
+        gain_v = load_vector(gain, "gain_v")
+        idx2 = load_list(offs2, "idx2")
+        for t in range(PACK - 1):
+            load_page(t)
+        idx3 = load_list(offs3, "idx3")
+        decay_v = load_vector(decay, "decay_v")
+        kept = {t: tile([P, T2], F32, f"kept{t}") for t in range(IN_PAGE, PACK)}
+        for t in kept:
+            nc.sync.dma_start(kept[t][:], page_rows[t])
+        w3_raw = tile([P, PACK, H], F32, "w3_raw", tag="tab_w0")
+        nc.sync.dma_start(w3_raw[:], w3.rearrange("(p i) m -> p i m", i=PACK))
+        load_page(PACK - 1)
+        gain2_v = load_vector(gain2, "gain2_v")
+        w4_w = tile([P, N], U32, "w4_w")
+        nc.sync.dma_start(w4_w[:].bitcast(I32), w4_words[0].rearrange("p n i -> p (n i)").bitcast(I32))
+        for q in range(4):
+            nc.sync.dma_start(
+                w4_s[32 * q : 32 * q + 4, :].bitcast(I32),
+                w4_scales[0, 4 * q : 4 * q + 4, :].bitcast(I32),
+            )
 
         def product(acc, jt, words, scales):
             cols = slice(P * jt, P * (jt + 1))
@@ -149,50 +162,56 @@ def tile_list_embankment_regrowth_scores_kernel(
         for a in range(PASSES):
             for u in range(2):
                 w1_b = tile([P, H // 2 * PACK], BF16, f"w1_b{a}{u}")
-                weave(nc.vector.tensor_copy, w1_b[:], w1_raw[a][u][:])
+                weave(nc.vector.tensor_copy if (a, u) == (1, 1) else nc.scalar.copy, w1_b[:], w1_raw[a][u][:])
                 nc.vector.quantize_mx(
                     out=w1_w[a][:, halves[u]].bitcast(FP8X4), scales=w1_s[a][:, halves[u]], in_=w1_b[:]
                 )
 
         h = [tile([P, S], F32, f"h{t}") for t in range(PACK)]
+        lin, bent = [], []
+
+        def make_h(t, tiles):
+            bank = psum.tile([P, len(tiles), P], F32, name="h_acc", tag="tr")
+            terms = [(n, src[jt]) for src in (lin, bent) for n, jt in enumerate(tiles)]
+            for k, (n, src) in enumerate(terms):
+                nc.tensor.matmul(bank[:, n, :], src[:, t, :], ident[:], start=(k == 0),
+                                 stop=(k == len(terms) - 1), is_transpose=True)
+            nc.scalar.activation(
+                out=h[t][:, P * tiles[0] : P * (tiles[-1] + 1)], in_=bank[:].rearrange("p a j -> p (a j)"),
+                func=ACT.Copy, scale=gain_v[:, t : t + 1],
+            )
+
+        w1_raw_tags = ["w1_raw10", "w1_raw11", "w1_raw00", "w1_raw01"]
         for c in range(CHUNKS):
-            lin, bent = [], []
+            lin_c = tile([P, 2, PACK, P], F32, f"lin{c}", tag=w1_raw_tags[c])
+            if c % 2 == 0:
+                bent_c = tile([P, 4, PACK, P], F32, f"bent{c}", tag=("tab_w1" if c == 0 else None))
             for jj in range(2):
-                acc = psum.tile([P, H], F32, name="lin_acc", tag="mm0", bufs=2)
+                acc = psum.tile([P, H], F32, name="lin_acc", tag=f"mm{2 * (c % 2) + jj}", bufs=1)
                 product(acc, 2 * c + jj, [w2_w[:, a, :].bitcast(FP4X4) for a in range(PASSES)],
                         [w2_s[:, a, :] for a in range(PASSES)])
-                lin_t = tile([P, PACK, P], F32, f"lin{c}{jj}")
                 nc.scalar.activation(
-                    out=lin_t[:], in_=acc[:].rearrange("j (p t) -> j t p", t=PACK), func=ACT.Copy
+                    out=lin_c[:, jj], in_=acc[:].rearrange("j (p t) -> j t p", t=PACK), func=ACT.Copy
                 )
-                lin.append(lin_t)
+                lin.append(lin_c[:, jj])
             for jj in range(2):
-                acc = psum.tile([P, H], F32, name="bent_acc", tag="mm1", bufs=2)
+                acc = psum.tile([P, H], F32, name="bent_acc", tag=f"mm{2 * (1 - c % 2) + jj}", bufs=1)
                 product(acc, 2 * c + jj, [w1_w[a][:].bitcast(FP8X4) for a in range(PASSES)],
                         [w1_s[a][:] for a in range(PASSES)])
-                bent_t = tile([P, PACK, P], F32, "bent", bufs=4)
+                dst = bent_c[:, 2 * (c % 2) + jj]
                 nc.scalar.activation(
-                    out=bent_t[:], in_=acc[:].rearrange("j (p t) -> j t p", t=PACK), func=ACT.Tanh
+                    out=dst, in_=acc[:].rearrange("j (p t) -> j t p", t=PACK), func=ACT.Tanh
                 )
-                bent.append(bent_t)
-            for pair in range(2):
-                bank = psum.tile([P, 2, CHUNK], F32, name="h_acc", tag="tr")
-                for tt in range(2):
-                    t = 2 * pair + tt
-                    for jj in range(2):
-                        dst = bank[:, tt, P * jj : P * (jj + 1)]
-                        nc.tensor.matmul(dst, lin[jj][:, t, :], ident[:],
-                                         start=True, stop=False, is_transpose=True)
-                        nc.tensor.matmul(dst, bent[jj][:, t, :], ident[:],
-                                         start=False, stop=True, is_transpose=True)
-                for tt in range(2):
-                    t = 2 * pair + tt
-                    nc.scalar.activation(
-                        out=h[t][:, CHUNK * c : CHUNK * (c + 1)], in_=bank[:, tt, :],
-                        func=ACT.Copy, scale=gain_v[:, t : t + 1],
-                    )
+                bent.append(dst)
+            make_h(0, [2 * c, 2 * c + 1])
+            if c % 2 == 1:
+                make_h(1, list(range(2 * c - 2, 2 * c + 2)))
+        for t in range(2, PACK):
+            for half in range(2):
+                make_h(t, list(range(4 * half, 4 * half + 4)))
 
-        old = [tile([P, PJ], F32, f"old{t}") for t in range(PACK)]
+        old = [tile([P, PJ], F32, f"old{t}") for t in range(IN_PAGE)]
+
         def read_old(t):
             nc.vector.tensor_copy(old[t][:], page[t][:].indirect(idx4[:]))
 
@@ -203,110 +222,145 @@ def tile_list_embankment_regrowth_scores_kernel(
             )
 
         read_old(0)
-        put(0, 0, 256)
+        put(0, 0, CHUNK)
         read_old(1)
-        put(0, 256, 256)
-        put(1, 0, 512)
-        read_old(2)
-        put(0, 512, 512)
-        put(1, 512, 512)
-        put(2, 0, 1024)
-        read_old(3)
-        put(3, 0, 1024)
+        put(0, CHUNK, CHUNK)
+        put(1, 0, S // 2)
+        put(0, 2 * CHUNK, CHUNK)
+        put(0, 3 * CHUNK, CHUNK)
+        put(1, S // 2, S // 2)
+        put(2, 0, S)
 
-        w3_b = tile([P, H * PACK], BF16, "w3_b")
+        w3_b = tile([P, H * PACK], BF16, "w3_b", tag="v_w1")
         nc.scalar.copy(
             out=w3_b[:].rearrange("p (t m i) -> p t m i", t=PACK, i=PACK),
             in_=w3_raw[:].rearrange("p i (m t) -> p t m i", t=PACK),
         )
-        w3_w = tile([P, H], U32, "w3_w")
+        w3_w = tile([P, H], U32, "w3_w", tag="h1")
         w3_s = tile([P, H], U8, "w3_s")
         nc.vector.quantize_mx(out=w3_w[:].bitcast(FP8X4), scales=w3_s[:], in_=w3_b[:])
 
         out_rows = out.rearrange("(a p) j -> p a j", p=P)
-        new, x, x_b, x_q, g, z, z_b = {}, {}, {}, {}, {}, {}, {}
+        new, was, x, x_b, g, z_b = {}, {}, {}, {}, {}, {}
 
-        def new_tag(c, t):
-            if c == 0:
-                return "new_b" if t == 3 else f"first{t}"
+        def gather(dst, window, lst, c):
+            nc.vector.tensor_copy(dst, window[:].indirect(entries(lst, CHUNK * c, CHUNK)))
+            return dst
+
+        def read_early(c):
+            buf = tile([P, 3, CHUNK], F32, f"early{c}", tag=("last0" if c == 1 else f"g{c % 2}"))
+            for t in kept:
+                was[c, t] = gather(buf[:, t - IN_PAGE, :], kept[t], idx4, c)
+            new[c, 0] = gather(buf[:, 2, :], page[0], idx3, c)
+
+        def read_mid(c):
+            buf = tile([P, 2, CHUNK], F32, f"mid{c}", tag="x_b")
+            for t in (1, 2):
+                new[c, t] = gather(buf[:, t - 1, :], page[t], idx3, c)
+
+        def read_late(c):
+            buf = tile([P, CHUNK], F32, f"late{c}", tag=("last0" if c == 0 else "z_b"))
+            new[c, 3] = gather(buf[:], page[3], idx3, c)
+
+        for c in range(CHUNKS):
+            for t in range(IN_PAGE):
+                was[c, t] = old[t][:, CHUNK * c : CHUNK * (c + 1)]
+
+        def x_rows(piece, t):
+            c, lo, width = piece
             if t == 0:
-                return "h3" if c == 1 else f"g{c % 2}"
-            return {1: "new_b", 2: "x_b", 3: "z_b"}[t]
+                x[piece] = tile([P, PACK, width], F32, f"x{c}_{lo}")
+            nc.vector.scalar_tensor_tensor(
+                x[piece][:, t, :], was[c, t][:, lo : lo + width], decay_v[:, t : t + 1],
+                new[c, t][:, lo : lo + width], ALU.mult, ALU.max,
+            )
 
-        def read_new(c, t):
-            new[c, t] = tile([P, CHUNK], F32, f"new{c}{t}", tag=new_tag(c, t))
-            nc.vector.tensor_copy(new[c, t][:], page[t][:].indirect(entries(idx3, CHUNK * c, CHUNK)))
+        def own_tag(piece, tag):
+            return tag if piece[2] == CHUNK else f"{tag}{piece[1]}"
 
-        def weave_engine(c):
-            return nc.vector.tensor_copy if c == CHUNKS - 1 else nc.scalar.copy
+        def make_x(piece, first=0):
+            for t in range(first, PACK):
+                x_rows(piece, t)
+            x_b[piece] = tile([P, piece[2] * PACK], BF16, "x_b", tag=own_tag(piece, "x_b"))
+            weave(nc.scalar.copy, x_b[piece][:], x[piece][:])
 
-        def make_x(c):
-            cols = slice(CHUNK * c, CHUNK * (c + 1))
-            x[c] = tile([P, PACK, CHUNK], F32, f"x{c}")
-            for t in range(PACK):
-                nc.vector.scalar_tensor_tensor(
-                    x[c][:, t, :], old[t][:, cols], decay_v[:, t : t + 1], new[c, t][:], ALU.mult, ALU.max
-                )
-            x_b[c] = tile([P, CHUNK * PACK], BF16, f"x_b{c}", tag="x_b")
-            weave(weave_engine(c), x_b[c][:], x[c][:])
-
-        def quantise(woven, name):
-            words = tile([P, CHUNK], U32, name + "_w", bufs=2)
-            scales = tile([P, CHUNK], U8, name + "_s", bufs=2)
+        def quantise(woven, name, width):
+            words = tile([P, width], U32, name + "_w", bufs=2)
+            scales = tile([P, width], U8, name + "_s", bufs=2)
             nc.vector.quantize_mx(out=words[:].bitcast(FP8X4), scales=scales[:], in_=woven[:])
             return words, scales
 
-        def stage_y(c):
-            x_w, x_s = quantise(x_b[c], "x")
-            g[c] = tile([P, PACK, CHUNK], F32, f"g{c}", tag=f"g{c % 2}")
-            for pair in range(2):
-                bank = psum.tile([P, 2, CHUNK], F32, name="y_acc", tag=f"mm{pair}", bufs=2)
-                for tt in range(2):
-                    m = slice(P * (2 * pair + tt), P * (2 * pair + tt + 1))
+        def stage_y(piece):
+            c, lo, width = piece
+            x_w, x_s = quantise(x_b[piece], "x", width)
+            g[piece] = tile([P, PACK, width], F32, "g", tag=own_tag(piece, f"g{c % 2}"))
+            per_bank = 512 // width
+            for b in range(PACK // per_bank):
+                bank = psum.tile([P, per_bank, width], F32, name="y_acc", tag=f"mm{2 * (c % 2) + b + lo // width}", bufs=1)
+                for tt in range(per_bank):
+                    m = slice(P * (per_bank * b + tt), P * (per_bank * b + tt + 1))
                     nc.tensor.matmul_mx(
                         out=bank[:, tt, :], lhsT=w3_w[:, m].bitcast(FP8X4), lhsT_scale=w3_s[:, m],
                         rhs=x_w[:].bitcast(FP8X4), rhs_scale=x_s[:], start=True, stop=True,
                     )
                 nc.scalar.activation(
-                    out=g[c][:, 2 * pair : 2 * pair + 2, :], in_=bank[:], func=ACT.Gelu_apprx_tanh
+                    out=g[piece][:, per_bank * b : per_bank * (b + 1), :], in_=bank[:],
+                    func=ACT.Gelu_apprx_tanh,
                 )
 
-        def make_z(c):
-            z[c] = tile([P, PACK, CHUNK], BF16, "z", bufs=2)
+        def make_z(piece, copy):
+            width = piece[2]
+            z = tile([P, PACK, width], BF16, "z", bufs=3)
             for t in range(PACK):
                 nc.vector.scalar_tensor_tensor(
-                    z[c][:, t, :], g[c][:, t, :], gain2_v[:, t : t + 1], x[c][:, t, :], ALU.mult, ALU.add
+                    z[:, t, :], g[piece][:, t, :], gain2_v[:, t : t + 1], x[piece][:, t, :], ALU.mult, ALU.add
                 )
-            z_b[c] = tile([P, CHUNK * PACK], BF16, f"z_b{c}", tag=("z_last" if c == CHUNKS - 1 else "z_b"))
-            weave(weave_engine(c), z_b[c][:], z[c][:])
+            z_b[piece] = tile([P, width * PACK], BF16, "z_b", tag=own_tag(piece, "z_b"))
+            weave(copy, z_b[piece][:], z[:])
 
-        def stage_out(c):
-            z_w, z_s = quantise(z_b[c], "z")
-            bank = psum.tile([P, N // P, CHUNK], F32, name="out_acc", tag="tr")
+        def stage_out(piece):
+            c, lo, width = piece
+            z_w, z_s = quantise(z_b[piece], "z", width)
+            bank = psum.tile([P, N // P, width], F32, name="out_acc", tag="tr")
             for a in range(N // P):
                 n = slice(P * a, P * (a + 1))
                 nc.tensor.matmul_mx(
                     out=bank[:, a, :], lhsT=w4_w[:, n].bitcast(FP8X4), lhsT_scale=w4_s[:, n],
                     rhs=z_w[:].bitcast(FP8X4), rhs_scale=z_s[:], start=True, stop=True,
                 )
-            res = tile([P, N // P, CHUNK], F32, "res", bufs=2)
+            res = tile([P, N // P, width], F32, "res", bufs=3)
             nc.scalar.copy(out=res[:], in_=bank[:])
-            nc.sync.dma_start(out_rows[:, :, CHUNK * c : CHUNK * (c + 1)], res[:])
+            first = CHUNK * c + lo
+            nc.sync.dma_start(out_rows[:, :, first : first + width], res[:])
 
-        for t in range(PACK):
-            read_new(0, t)
-        make_x(0)
+        whole = [(c, 0, CHUNK) for c in range(CHUNKS - 1)]
+        last = [(CHUNKS - 1, lo, CHUNK // 2) for lo in (0, CHUNK // 2)]
+
+        first_buf = tile([P, 5, CHUNK], F32, "first_buf")
+        for t in range(PACK - 1):
+            new[0, t] = gather(first_buf[:, t, :], page[t], idx3, 0)
+        for t in kept:
+            was[0, t] = gather(first_buf[:, 1 + t, :], kept[t], idx4, 0)
+        for t in range(PACK - 1):
+            x_rows(whole[0], t)
+        put(3, 0, S)
+        read_late(0)
+        make_x(whole[0], first=3)
         for c in range(1, CHUNKS):
-            read_new(c, 0)
-            read_new(c, 1)
-            stage_y(c - 1)
-            read_new(c, 2)
+            read_early(c)
+            stage_y(whole[c - 1])
+            read_mid(c)
             if c >= 2:
-                stage_out(c - 2)
-            read_new(c, 3)
-            make_x(c)
-            make_z(c - 1)
-        stage_y(CHUNKS - 1)
-        stage_out(CHUNKS - 2)
-        make_z(CHUNKS - 1)
-        stage_out(CHUNKS - 1)
+                stage_out(whole[c - 2])
+            read_late(c)
+            for piece in (last if c == CHUNKS - 1 else [whole[c]]):
+                make_x(piece)
+            if c < CHUNKS - 1:
+                make_z(whole[c - 1], nc.scalar.copy)
+        for piece in last:
+            stage_y(piece)
+        make_z(whole[-1], nc.scalar.copy)
+        for piece in last:
+            make_z(piece, nc.vector.tensor_copy)
+        for piece in [last[0], whole[-1], last[1]]:
+            stage_out(piece)

@@ -118,20 +118,32 @@ def tile_list_embankment_regrowth_scores_kernel(
                 )
 
         page = [tile([P, T2], F32, f"page{t}") for t in range(PACK)]
-        wg = [tile([P, S], F32, f"wg{t}") for t in range(PACK)]
         page_rows = page0.rearrange("(p t) c -> t p c", t=PACK)
-        wgs_rows = wgs.rearrange("(p t) j -> t p j", t=PACK)
+        wgs_rows = wgs.rearrange("(p t) j -> p t j", t=PACK)
+        wg = {}
 
         def load_page(t):
             nc.sync.dma_start(page[t][:], page_rows[t])
+
+        def load_wgs(t0, first, count):
+            piece = tile([P, 2, count], F32, f"wg{t0}_{first}")
             for q in (0, 2, 1, 3):
-                nc.sync.dma_start(wg[t][32 * q : 32 * (q + 1), :], wgs_rows[t])
+                nc.sync.dma_start(
+                    piece[32 * q : 32 * (q + 1)], wgs_rows[:, t0 : t0 + 2, first : first + count]
+                )
+            for t in (t0, t0 + 1):
+                for j in range(first, first + count, CHUNK):
+                    wg[t, j] = piece[:, t - t0, j - first :]
 
         idx4 = load_list(offs4, "idx4")
         gain_v = load_vector(gain, "gain_v")
         idx2 = load_list(offs2, "idx2")
-        for t in range(PACK - 1):
-            load_page(t)
+        load_page(0)
+        load_wgs(0, 0, S // 2)
+        load_page(1)
+        load_wgs(0, S // 2, S // 2)
+        load_page(2)
+        load_wgs(2, 0, S)
         idx3 = load_list(offs3, "idx3")
         decay_v = load_vector(decay, "decay_v")
         kept = {t: tile([P, T2], F32, f"kept{t}") for t in range(IN_PAGE, PACK)}
@@ -195,7 +207,7 @@ def tile_list_embankment_regrowth_scores_kernel(
                 )
                 lin.append(lin_c[:, jj])
             for jj in range(2):
-                acc = psum.tile([P, H], F32, name="bent_acc", tag=f"mm{2 * (1 - c % 2) + jj}", bufs=1)
+                acc = psum.tile([P, H], F32, name="bent_acc", tag=f"mm{2 * (c % 2) + jj}", bufs=1)
                 product(acc, 2 * c + jj, [w1_w[a][:].bitcast(FP8X4) for a in range(PASSES)],
                         [w1_s[a][:] for a in range(PASSES)])
                 dst = bent_c[:, 2 * (c % 2) + jj]
@@ -218,7 +230,7 @@ def tile_list_embankment_regrowth_scores_kernel(
         def put(t, first, count):
             cols = slice(first, first + count)
             nc.vector.tensor_tensor(
-                page[t][:].indirect(entries(idx2, first, count)), h[t][:, cols], wg[t][:, cols], ALU.mult
+                page[t][:].indirect(entries(idx2, first, count)), h[t][:, cols], wg[t, first][:, :count], ALU.mult
             )
 
         read_old(0)

@@ -23,7 +23,7 @@ PASSES = K // (P * PACK)
 CHUNK = 256
 CHUNKS = PJ // CHUNK
 LIST_ROWS = 16
-IN_PAGE = 2
+IN_PAGE = 3
 
 
 def weave(copy, dst, src):
@@ -139,10 +139,10 @@ def tile_list_embankment_regrowth_scores_kernel(
         gain_v = load_vector(gain, "gain_v")
         idx2 = load_list(offs2, "idx2")
         load_page(0)
-        load_wgs(0, 0, S // 2)
         load_page(1)
-        load_wgs(0, S // 2, S // 2)
         load_page(2)
+        load_wgs(0, 0, S // 2)
+        load_wgs(0, S // 2, S // 2)
         load_wgs(2, 0, S)
         idx3 = load_list(offs3, "idx3")
         decay_v = load_vector(decay, "decay_v")
@@ -234,8 +234,9 @@ def tile_list_embankment_regrowth_scores_kernel(
             )
 
         read_old(0)
-        put(0, 0, CHUNK)
         read_old(1)
+        read_old(2)
+        put(0, 0, CHUNK)
         put(0, CHUNK, CHUNK)
         put(1, 0, S // 2)
         put(0, 2 * CHUNK, CHUNK)
@@ -261,14 +262,13 @@ def tile_list_embankment_regrowth_scores_kernel(
 
         def read_early(c):
             buf = tile([P, 3, CHUNK], F32, f"early{c}", tag=("last0" if c == 1 else f"g{c % 2}"))
-            for t in kept:
-                was[c, t] = gather(buf[:, t - IN_PAGE, :], kept[t], idx4, c)
-            new[c, 0] = gather(buf[:, 2, :], page[0], idx3, c)
+            was[c, 3] = gather(buf[:, 2, :], kept[3], idx4, c)
+            for t in (0, 1):
+                new[c, t] = gather(buf[:, t, :], page[t], idx3, c)
 
         def read_mid(c):
-            buf = tile([P, 2, CHUNK], F32, f"mid{c}", tag="x_b")
-            for t in (1, 2):
-                new[c, t] = gather(buf[:, t - 1, :], page[t], idx3, c)
+            buf = tile([P, CHUNK], F32, f"mid{c}", tag="x_b")
+            new[c, 2] = gather(buf[:], page[2], idx3, c)
 
         def read_late(c):
             buf = tile([P, CHUNK], F32, f"late{c}", tag=("last0" if c == 0 else "z_b"))
@@ -348,11 +348,11 @@ def tile_list_embankment_regrowth_scores_kernel(
         whole = [(c, 0, CHUNK) for c in range(CHUNKS - 1)]
         last = [(CHUNKS - 1, lo, CHUNK // 2) for lo in (0, CHUNK // 2)]
 
-        first_buf = tile([P, 5, CHUNK], F32, "first_buf")
+        first_buf = tile([P, 4, CHUNK], F32, "first_buf")
         for t in range(PACK - 1):
             new[0, t] = gather(first_buf[:, t, :], page[t], idx3, 0)
         for t in kept:
-            was[0, t] = gather(first_buf[:, 1 + t, :], kept[t], idx4, 0)
+            was[0, t] = gather(first_buf[:, t, :], kept[t], idx4, 0)
         for t in range(PACK - 1):
             x_rows(whole[0], t)
         put(3, 0, S)
@@ -371,8 +371,9 @@ def tile_list_embankment_regrowth_scores_kernel(
                 make_z(whole[c - 1], nc.scalar.copy)
         for piece in last:
             stage_y(piece)
-        make_z(whole[-1], nc.scalar.copy)
+        make_z(whole[-1], nc.vector.tensor_copy)
+        stage_out(whole[-1])
+        make_z(last[0], nc.scalar.copy)
+        make_z(last[1], nc.vector.tensor_copy)
         for piece in last:
-            make_z(piece, nc.vector.tensor_copy)
-        for piece in [last[0], whole[-1], last[1]]:
             stage_out(piece)

from contextlib import ExitStack

import concourse.mybir as mybir
from concourse.masks import make_identity

K, H, N, T, S, T2, PJ = 1024, 512, 256, 2048, 1024, 2048, 1024
FLOPS = 2952790016

F32 = mybir.dt.float32
BF16 = mybir.dt.bfloat16
I32 = mybir.dt.int32
U32 = mybir.dt.uint32
U16 = mybir.dt.uint16
U8 = mybir.dt.uint8
FP8X4 = mybir.dt.float8_e4m3fn_x4
FP4X4 = mybir.dt.float4_e2m1fn_x4
ALU = mybir.AluOpType
ACT = mybir.ActivationFunctionType

P = 128
PACK = 4
PASSES = K // (P * PACK)
CHUNK = 256
CHUNKS = PJ // CHUNK
LIST_ROWS = 16
IN_PAGE = 3


def weave(copy, dst, src):
    copy(
        out=dst.rearrange("p (c k i) -> p c i k", k=4, i=PACK),
        in_=src.rearrange("p i (c k) -> p c i k", k=4),
    )


def tile_list_embankment_regrowth_scores_kernel(
    tc, tab_words, tab_scales, offs, offs2, offs3, offs4, w1, w2_words, w2_scales,
    gain, wgs, page0, decay, w3, gain2, w4_words, w4_scales, out,
):
    nc = tc.nc
    with ExitStack() as ctx:
        keep = ctx.enter_context(tc.tile_pool(name="keep", bufs=1))
        psum = ctx.enter_context(tc.psum_pool(name="psum", bufs=4))

        def tile(shape, dtype, name, tag=None, bufs=None):
            return keep.tile(shape, dtype, name=name, tag=tag or name, bufs=bufs, align_bytes=64)

        def load_list(src, name):
            lst = tile([P, S // LIST_ROWS], U16, name)
            nc.sync.dma_start(lst[:], src)
            return lst

        def entries(lst, first, count):
            return lst[:, first // LIST_ROWS : (first + count) // LIST_ROWS]

        idx = load_list(offs, "idx")
        tab_s = tile([P, T], U8, "tab_s")
        scale_rows = tab_scales.rearrange("a q t -> (a q) t").bitcast(I32)
        nc.sync.dma_start(tab_s[0:32, :].bitcast(I32), scale_rows)
        for q in range(1, 4):
            nc.sync.dma_start(
                tab_s[32 * q : 32 * (q + 1), :].bitcast(I32),
                scale_rows[4 * q : 4 * q + 4, :].unsqueeze(0).to_broadcast([8, 4, T // 4]),
            )
        tab_w = [tile([P, T], U32, f"tab_w{a}") for a in range(PASSES)]

        def load_words(a):
            nc.sync.dma_start(
                tab_w[a][:].bitcast(I32), tab_words[a].rearrange("p n i -> p (n i)").bitcast(I32)
            )

        halves = [slice(0, H // 2), slice(H // 2, H)]
        w1_raw = [[tile([P, PACK, H // 2], F32, f"w1_raw{a}{u}") for u in range(2)] for a in range(PASSES)]

        def load_w1(a):
            rows = w1[512 * a : 512 * (a + 1), :].rearrange("(p i) c -> p i c", i=PACK)
            for u in range(2):
                nc.sync.dma_start(w1_raw[a][u][:], rows[:, :, halves[u]])

        def load_vector(src, name):
            vec = tile([P, PACK], F32, name)
            nc.sync.dma_start(vec[:], src.rearrange("(p t) -> p t", t=PACK))
            return vec

        load_words(0)
        load_w1(0)
        load_words(1)
        w2_s = tile([P, PASSES, H], U8, "w2_s")
        nc.vector.memset(w2_s[:].bitcast(I32), 0)
        for q in range(4):
            nc.sync.dma_start(
                w2_s[32 * q : 32 * q + 4].bitcast(I32),
                w2_scales[:, 4 * q : 4 * q + 4, :].rearrange("a r c -> r a c").bitcast(I32),
            )
        w2_w = tile([P, PASSES, 2 * H], U8, "w2_w")
        nc.sync.dma_start(w2_w[:].bitcast(I32), w2_words.rearrange("a p c -> p a c").bitcast(I32))
        v_s1 = tile([P, S], U8, "v_s1")
        nc.vector.memset(v_s1[:].bitcast(I32), 0)
        w4_s = tile([P, N], U8, "w4_s")
        nc.vector.memset(w4_s[:].bitcast(I32), 0)
        ident = tile([P, P], F32, "ident")
        make_identity(nc, ident[:])
        load_w1(1)

        v_s0 = tile([P, S], U8, "v_s0")
        nc.vector.tensor_copy(v_s0[:], tab_s[:].indirect(idx[:]))
        for q in range(4):
            nc.gpsimd.dma_start(
                v_s1[32 * q : 32 * q + 4, :].bitcast(I32),
                v_s0[16 + 4 * q : 16 + 4 * q + 4, :].bitcast(I32),
            )
        v_s = [v_s0, v_s1]
        v_w = [tile([P, S], U32, f"v_w{a}") for a in range(PASSES)]
        for a in range(PASSES):
            for j0 in range(0, S, 512):
                nc.vector.tensor_copy(
                    v_w[a][:, j0 : j0 + 512], tab_w[a][:].indirect(entries(idx, j0, 512))
                )

        page = [tile([P, T2], F32, f"page{t}") for t in range(PACK)]
        page_rows = page0.rearrange("(p t) c -> t p c", t=PACK)
        wgs_rows = wgs.rearrange("(p t) j -> p t j", t=PACK)
        wg = {}

        def load_page(t):
            nc.sync.dma_start(page[t][:], page_rows[t])

        def load_wgs(t0, first, count):
            piece = tile([P, 2, count], F32, f"wg{t0}_{first}")
            for q in (0, 2, 1, 3):
                nc.sync.dma_start(
                    piece[32 * q : 32 * (q + 1)], wgs_rows[:, t0 : t0 + 2, first : first + count]
                )
            for t in (t0, t0 + 1):
                for j in range(first, first + count, CHUNK):
                    wg[t, j] = piece[:, t - t0, j - first :]

        idx4 = load_list(offs4, "idx4")
        gain_v = load_vector(gain, "gain_v")
        idx2 = load_list(offs2, "idx2")
        load_page(0)
        load_page(1)
        load_page(2)
        load_wgs(0, 0, S // 2)
        load_wgs(0, S // 2, S // 2)
        load_wgs(2, 0, S)
        idx3 = load_list(offs3, "idx3")
        decay_v = load_vector(decay, "decay_v")
        kept = {t: tile([P, T2], F32, f"kept{t}") for t in range(IN_PAGE, PACK)}
        for t in kept:
            nc.sync.dma_start(kept[t][:], page_rows[t])
        w3_raw = tile([P, PACK, H], F32, "w3_raw", tag="tab_w0")
        nc.sync.dma_start(w3_raw[:], w3.rearrange("(p i) m -> p i m", i=PACK))
        load_page(PACK - 1)
        gain2_v = load_vector(gain2, "gain2_v")
        w4_w = tile([P, N], U32, "w4_w")
        nc.sync.dma_start(w4_w[:].bitcast(I32), w4_words[0].rearrange("p n i -> p (n i)").bitcast(I32))
        for q in range(4):
            nc.sync.dma_start(
                w4_s[32 * q : 32 * q + 4, :].bitcast(I32),
                w4_scales[0, 4 * q : 4 * q + 4, :].bitcast(I32),
            )

        def product(acc, jt, words, scales):
            cols = slice(P * jt, P * (jt + 1))
            for a in range(PASSES):
                nc.tensor.matmul_mx(
                    out=acc[:], lhsT=v_w[a][:, cols].bitcast(FP8X4), lhsT_scale=v_s[a][:, cols],
                    rhs=words[a], rhs_scale=scales[a], start=(a == 0), stop=(a == PASSES - 1),
                )

        w1_w = [tile([P, H], U32, f"w1_w{a}") for a in range(PASSES)]
        w1_s = [tile([P, H], U8, f"w1_s{a}") for a in range(PASSES)]
        for a in range(PASSES):
            for u in range(2):
                w1_b = tile([P, H // 2 * PACK], BF16, f"w1_b{a}{u}")
                weave(nc.vector.tensor_copy if (a, u) == (1, 1) else nc.scalar.copy, w1_b[:], w1_raw[a][u][:])
                nc.vector.quantize_mx(
                    out=w1_w[a][:, halves[u]].bitcast(FP8X4), scales=w1_s[a][:, halves[u]], in_=w1_b[:]
                )

        h = [tile([P, S], F32, f"h{t}") for t in range(PACK)]
        lin, bent = [], []

        def make_h(t, tiles):
            bank = psum.tile([P, len(tiles), P], F32, name="h_acc", tag="tr")
            terms = [(n, src[jt]) for src in (lin, bent) for n, jt in enumerate(tiles)]
            for k, (n, src) in enumerate(terms):
                nc.tensor.matmul(bank[:, n, :], src[:, t, :], ident[:], start=(k == 0),
                                 stop=(k == len(terms) - 1), is_transpose=True)
            nc.scalar.activation(
                out=h[t][:, P * tiles[0] : P * (tiles[-1] + 1)], in_=bank[:].rearrange("p a j -> p (a j)"),
                func=ACT.Copy, scale=gain_v[:, t : t + 1],
            )

        w1_raw_tags = ["w1_raw10", "w1_raw11", "w1_raw00", "w1_raw01"]
        for c in range(CHUNKS):
            lin_c = tile([P, 2, PACK, P], F32, f"lin{c}", tag=w1_raw_tags[c])
            if c % 2 == 0:
                bent_c = tile([P, 4, PACK, P], F32, f"bent{c}", tag=("tab_w1" if c == 0 else None))
            for jj in range(2):
                acc = psum.tile([P, H], F32, name="lin_acc", tag=f"mm{2 * (c % 2) + jj}", bufs=1)
                product(acc, 2 * c + jj, [w2_w[:, a, :].bitcast(FP4X4) for a in range(PASSES)],
                        [w2_s[:, a, :] for a in range(PASSES)])
                nc.scalar.activation(
                    out=lin_c[:, jj], in_=acc[:].rearrange("j (p t) -> j t p", t=PACK), func=ACT.Copy
                )
                lin.append(lin_c[:, jj])
            for jj in range(2):
                acc = psum.tile([P, H], F32, name="bent_acc", tag=f"mm{2 * (c % 2) + jj}", bufs=1)
                product(acc, 2 * c + jj, [w1_w[a][:].bitcast(FP8X4) for a in range(PASSES)],
                        [w1_s[a][:] for a in range(PASSES)])
                dst = bent_c[:, 2 * (c % 2) + jj]
                nc.scalar.activation(
                    out=dst, in_=acc[:].rearrange("j (p t) -> j t p", t=PACK), func=ACT.Tanh
                )
                bent.append(dst)
            make_h(0, [2 * c, 2 * c + 1])
            if c % 2 == 1:
                make_h(1, list(range(2 * c - 2, 2 * c + 2)))
        for t in range(2, PACK):
            for half in range(2):
                make_h(t, list(range(4 * half, 4 * half + 4)))

        old = [tile([P, PJ], F32, f"old{t}") for t in range(IN_PAGE)]

        def read_old(t):
            nc.vector.tensor_copy(old[t][:], page[t][:].indirect(idx4[:]))

        def put(t, first, count):
            cols = slice(first, first + count)
            nc.vector.tensor_tensor(
                page[t][:].indirect(entries(idx2, first, count)), h[t][:, cols], wg[t, first][:, :count], ALU.mult
            )

        read_old(0)
        read_old(1)
        read_old(2)
        put(0, 0, CHUNK)
        put(0, CHUNK, CHUNK)
        put(1, 0, S // 2)
        put(0, 2 * CHUNK, CHUNK)
        put(0, 3 * CHUNK, CHUNK)
        put(1, S // 2, S // 2)
        put(2, 0, S)

        w3_b = tile([P, H * PACK], BF16, "w3_b", tag="v_w1")
        nc.scalar.copy(
            out=w3_b[:].rearrange("p (t m i) -> p t m i", t=PACK, i=PACK),
            in_=w3_raw[:].rearrange("p i (m t) -> p t m i", t=PACK),
        )
        w3_w = tile([P, H], U32, "w3_w", tag="h1")
        w3_s = tile([P, H], U8, "w3_s")
        nc.vector.quantize_mx(out=w3_w[:].bitcast(FP8X4), scales=w3_s[:], in_=w3_b[:])

        out_rows = out.rearrange("(a p) j -> p a j", p=P)
        new, was, x, x_b, g, z_b = {}, {}, {}, {}, {}, {}

        def gather(dst, window, lst, c):
            nc.vector.tensor_copy(dst, window[:].indirect(entries(lst, CHUNK * c, CHUNK)))
            return dst

        def read_early(c):
            buf = tile([P, 3, CHUNK], F32, f"early{c}", tag=("last0" if c == 1 else f"g{c % 2}"))
            was[c, 3] = gather(buf[:, 2, :], kept[3], idx4, c)
            for t in (0, 1):
                new[c, t] = gather(buf[:, t, :], page[t], idx3, c)

        def read_mid(c):
            buf = tile([P, CHUNK], F32, f"mid{c}", tag="x_b")
            new[c, 2] = gather(buf[:], page[2], idx3, c)

        def read_late(c):
            buf = tile([P, CHUNK], F32, f"late{c}", tag=("last0" if c == 0 else "z_b"))
            new[c, 3] = gather(buf[:], page[3], idx3, c)

        for c in range(CHUNKS):
            for t in range(IN_PAGE):
                was[c, t] = old[t][:, CHUNK * c : CHUNK * (c + 1)]

        def x_rows(piece, t):
            c, lo, width = piece
            if t == 0:
                x[piece] = tile([P, PACK, width], F32, f"x{c}_{lo}")
            nc.vector.scalar_tensor_tensor(
                x[piece][:, t, :], was[c, t][:, lo : lo + width], decay_v[:, t : t + 1],
                new[c, t][:, lo : lo + width], ALU.mult, ALU.max,
            )

        def own_tag(piece, tag):
            return tag if piece[2] == CHUNK else f"{tag}{piece[1]}"

        def make_x(piece, first=0):
            for t in range(first, PACK):
                x_rows(piece, t)
            x_b[piece] = tile([P, piece[2] * PACK], BF16, "x_b", tag=own_tag(piece, "x_b"))
            weave(nc.scalar.copy, x_b[piece][:], x[piece][:])

        def quantise(woven, name, width):
            words = tile([P, width], U32, name + "_w", bufs=2)
            scales = tile([P, width], U8, name + "_s", bufs=2)
            nc.vector.quantize_mx(out=words[:].bitcast(FP8X4), scales=scales[:], in_=woven[:])
            return words, scales

        def stage_y(piece):
            c, lo, width = piece
            x_w, x_s = quantise(x_b[piece], "x", width)
            g[piece] = tile([P, PACK, width], F32, "g", tag=own_tag(piece, f"g{c % 2}"))
            per_bank = 512 // width
            for b in range(PACK // per_bank):
                bank = psum.tile([P, per_bank, width], F32, name="y_acc", tag=f"mm{2 * (c % 2) + b + lo // width}", bufs=1)
                for tt in range(per_bank):
                    m = slice(P * (per_bank * b + tt), P * (per_bank * b + tt + 1))
                    nc.tensor.matmul_mx(
                        out=bank[:, tt, :], lhsT=w3_w[:, m].bitcast(FP8X4), lhsT_scale=w3_s[:, m],
                        rhs=x_w[:].bitcast(FP8X4), rhs_scale=x_s[:], start=True, stop=True,
                    )
                nc.scalar.activation(
                    out=g[piece][:, per_bank * b : per_bank * (b + 1), :], in_=bank[:],
                    func=ACT.Gelu_apprx_tanh,
                )

        def make_z(piece, copy):
            width = piece[2]
            z = tile([P, PACK, width], BF16, "z", bufs=3)
            for t in range(PACK):
                nc.vector.scalar_tensor_tensor(
                    z[:, t, :], g[piece][:, t, :], gain2_v[:, t : t + 1], x[piece][:, t, :], ALU.mult, ALU.add
                )
            z_b[piece] = tile([P, width * PACK], BF16, "z_b", tag=own_tag(piece, "z_b"))
            weave(copy, z_b[piece][:], z[:])

        def stage_out(piece):
            c, lo, width = piece
            z_w, z_s = quantise(z_b[piece], "z", width)
            bank = psum.tile([P, N // P, width], F32, name="out_acc", tag="tr")
            for a in range(N // P):
                n = slice(P * a, P * (a + 1))
                nc.tensor.matmul_mx(
                    out=bank[:, a, :], lhsT=w4_w[:, n].bitcast(FP8X4), lhsT_scale=w4_s[:, n],
                    rhs=z_w[:].bitcast(FP8X4), rhs_scale=z_s[:], start=True, stop=True,
                )
            res = tile([P, N // P, width], F32, "res", bufs=3)
            nc.scalar.copy(out=res[:], in_=bank[:])
            first = CHUNK * c + lo
            nc.sync.dma_start(out_rows[:, :, first : first + width], res[:])

        whole = [(c, 0, CHUNK) for c in range(CHUNKS - 1)]
        last = [(CHUNKS - 1, lo, CHUNK // 2) for lo in (0, CHUNK // 2)]

        first_buf = tile([P, 4, CHUNK], F32, "first_buf")
        for t in range(PACK - 1):
            new[0, t] = gather(first_buf[:, t, :], page[t], idx3, 0)
        for t in kept:
            was[0, t] = gather(first_buf[:, t, :], kept[t], idx4, 0)
        for t in range(PACK - 1):
            x_rows(whole[0], t)
        put(3, 0, S)
        read_late(0)
        make_x(whole[0], first=3)
        for c in range(1, CHUNKS):
            read_early(c)
            stage_y(whole[c - 1])
            read_mid(c)
            if c >= 2:
                stage_out(whole[c - 2])
            read_late(c)
            for piece in (last if c == CHUNKS - 1 else [whole[c]]):
                make_x(piece)
            if c < CHUNKS - 1:
                make_z(whole[c - 1], nc.scalar.copy)
        for piece in last:
            stage_y(piece)
        make_z(whole[-1], nc.vector.tensor_copy)
        stage_out(whole[-1])
        make_z(last[0], nc.scalar.copy)
        make_z(last[1], nc.vector.tensor_copy)
        for piece in last:
            stage_out(piece)
